import numpy as np
CORES = [23,39,55,63,87,103,111,127,18,34,50,58,82,98,106,122]
N = 16
def setup_inputs(rng):
    dy = rng.standard_normal((N, 128, N * 128), dtype=np.float32)
    dyt = np.concatenate([dy[:, :, 128 * j:128 * j + 128].transpose(0, 2, 1) for j in range(N)], axis=2)
    return {"x": rng.standard_normal((N, 128, 128), dtype=np.float32), "wt": rng.standard_normal((N, 128, 128), dtype=np.float32), "dy": dy, "dyt": dyt}
def setup_inputs_big(rng):
    d = setup_inputs(rng)
    for k in ("x", "wt", "dy", "dyt"): d[k] = (d[k].astype(np.float32) * 1024.0).astype(d[k].dtype)
    return d
def setup_inputs_small(rng):
    d = setup_inputs(rng)
    for k in ("x", "wt", "dy", "dyt"): d[k] = (d[k].astype(np.float32) * (1 / 1024.0)).astype(d[k].dtype)
    return d
def setup_inputs_apart(rng):
    d = setup_inputs(rng)
    f = (10.0 ** rng.permutation(np.linspace(-1.5, 1.5, N))).astype(np.float32).reshape(N, 1, 1)
    for k in ("x", "wt", "dy", "dyt"): d[k] = (d[k].astype(np.float32) * f).astype(d[k].dtype)
    return d
def tie_inputs(x):
    x = dict(x)
    x["dyt"] = np.concatenate([x["dy"][:, :, 128 * j:128 * j + 128].transpose(0, 2, 1) for j in range(N)], axis=2)
    return x
def reference(x, wt, dy, dyt):
    X, WT, DY, DYT = x.astype(np.float64), wt.astype(np.float64), dy.astype(np.float64), dyt.astype(np.float64)
    dx = np.zeros((N, 128, 128)); dw = np.zeros((N, 128, 128))
    for r in range(N):
        for j in range(N):
            dx[r] += WT[j].T @ DY[j][:, 128 * r:128 * r + 128]
            dw[r] += X[j].T @ DYT[r][:, 128 * j:128 * j + 128]
    return {"dx": dx.astype(np.float32 if x.dtype != np.float64 else np.float64), "dw": dw.astype(np.float32 if x.dtype != np.float64 else np.float64)}

@@ -1,0 +1,195 @@
+from concourse.bass import DstId, RemoteDMATransfer
+from concourse.mybir import AluOpType
+
+B = 128
+NB = 8
+XO = B + NB * B
+HALF = XO + B
+
+SCRATCH = {
+    "exs": ("sbuf", [128, HALF], "float32"),
+    "exr": ("sbuf", [128, HALF], "float32"),
+    "dyo": ("sbuf", [128, NB * B], "float32"),
+    "dts": ("sbuf", [128, 16 * B], "float32"),
+    "xl": ("sbuf", [128, 7 * B], "float32"),
+    "xf": ("sbuf", [128, 7 * B], "float32"),
+    "ps": ("sbuf", [128, 7 * B], "float32"),
+    "dl": ("sbuf", [128, 7 * B], "float32"),
+    "dxo": ("sbuf", [128, B], "float32"),
+    "dwo": ("sbuf", [128, B], "float32"),
+    "b0": ("psum", [128, 512], "float32"),
+    "b1": ("psum", [128, 512], "float32"),
+    "b2": ("psum", [128, 512], "float32"),
+}
+SEMAPHORES = (["lx", "lw", "lp0", "lp1", "lo0", "lo1", "lt0", "lt1", "lt2", "lt3", "gate", "e0", "e1", "fa", "fb",
+               "pe0", "pe1", "pe2", "ev0", "ev1", "vs", "dwv", "sdx", "sdw", "sent"]
+              + ["x%d" % i for i in range(8)] + ["p%d" % i for i in range(8)])
+
+
+def _bits(m):
+    return [b for b in range(m.bit_length()) if (m >> b) & 1]
+
+
+def _mk(bs):
+    m = 0
+    for b in bs:
+        m |= 1 << b
+    return m
+
+
+def _runs(ranks, lo, hi):
+    out, t = [], lo
+    while t < hi:
+        n = 1
+        while t + n < hi and ranks[t + n] == ranks[t] + n:
+            n += 1
+        out.append((t, ranks[t], n))
+        t += n
+    return out
+
+
+def rank_program(g, core, T, topo):
+    rank = T.rank_of(core)
+    if rank is None:
+        return
+    S = T.sem
+    sy, sc, pe, ve = g.sync, g.scalar, g.tensor, g.vector
+    cores = list(T.cores)
+    chips = []
+    for c in cores:
+        if topo.chip(c) not in chips:
+            chips.append(topo.chip(c))
+    Q = len(chips)
+    q = chips.index(topo.chip(core))
+
+    def at(qi, die):
+        return [c for c in cores if topo.chip(c) == chips[qi % Q] and topo.die(c) == die][0]
+
+    partner = [c for c in cores if topo.chip(c) == topo.chip(core) and c != core][0]
+    peers = [at(q + k, topo.die(core)) for k in range(Q)]
+    ppeers = [at(q + k, topo.die(partner)) for k in range(Q)]
+    order = list(range(1, Q)) + [0]
+    own_r = [T.rank_of(peers[k]) for k in order]
+    par_r = [T.rank_of(ppeers[k]) for k in order]
+
+    off = topo.mask(core, partner)
+    for k in range(1, Q):
+        assert topo.may_write(core, peers[k])
+        off &= topo.mask(core, peers[k])
+    onl = topo.mask(core, partner) & ~off
+    if len(_bits(onl)) not in (1, 2, 4, 8, 16):
+        onl = topo.mask(core, partner)
+    ob = _bits(off)
+    ne, nl = len(ob), len(_bits(onl))
+    e4 = ne // 4
+    pbits = [ob[i * e4:(i + 1) * e4] for i in range(4)] + [ob[0:2 * e4], ob[2 * e4:3 * e4], ob[3 * e4:4 * e4]]
+    prid, ppid, _ = topo.addr(partner)
+
+    def load(qu, dst, base, ranks, lo, hi, sem):
+        rs = _runs(ranks, lo, hi)
+        for (t, r, n) in rs:
+            qu.dma_start(dst[:, base + t * B:base + (t + n) * B], T.dy[:, r * B:(r + n) * B]).then_inc(S[sem], 16)
+        return 16 * len(rs)
+
+    terms = [(T.exs[:, XO:XO + B], rank, "lx", 16)]
+    for k in range(1, Q):
+        terms.append((T.xl[:, (k - 1) * B:k * B], T.rank_of(peers[Q - k]), "x%d" % ((q - k) % Q), ne))
+    terms.append((T.exr[:, XO:XO + B], T.rank_of(partner), "e1", nl))
+    for k in range(1, Q):
+        terms.append((T.xf[:, (k - 1) * B:k * B], T.rank_of(ppeers[Q - k]), "fa" if k <= 4 else "fb", nl))
+    corder = []
+    for t in terms:
+        if t[1] // 4 not in corder:
+            corder.append(t[1] // 4)
+
+    def load_t(qu, i):
+        c = corder[i]
+        qu.dma_start(T.dts[:, c * 512:(c + 1) * 512], T.dyt[:, c * 512:(c + 1) * 512]).then_inc(S["lt%d" % i], 16)
+
+    sy.dma_start(T.exs[:, XO:XO + B], T.x[:, :]).then_inc(S.lx, 16)
+    sc.dma_start(T.exs[:, 0:B], T.wt[:, :]).then_inc(S.lw, 16)
+    n_p0 = load(sy, T.exs, B, par_r, 0, 4, "lp0")
+    n_p1 = load(sc, T.exs, B, par_r, 4, 8, "lp1")
+    n_o0 = load(sy, T.dyo, 0, own_r, 0, 4, "lo0")
+    n_o1 = load(sc, T.dyo, 0, own_r, 4, 8, "lo1")
+    load_t(sy, 0)
+    load_t(sc, 1)
+    sy.wait_ge(S.gate, 1)
+    load_t(sy, 2)
+    sc.wait_ge(S.gate, 1)
+    load_t(sc, 3)
+    sy.wait_ge(S.vs, Q - 1)
+    sy.dma_start(T.dx[:, :], T.dxo[:, :]).then_inc(S.sdx, 16)
+    sc.wait_ge(S.dwv, 1)
+    sc.dma_start(T.dw[:, :], T.dwo[:, :]).then_inc(S.sdw, 16)
+
+    pe.wait_ge(S.lw, 16)
+    pe.wait_ge(S.lo0, n_o0)
+    pe.matmul(T.b0[:, :], T.exs[:, 0:B], T.dyo[:, 0:512], True, False)
+    pe.wait_ge(S.lo1, n_o1)
+    pe.matmul(T.b1[:, :], T.exs[:, 0:B], T.dyo[:, 512:1024], True, False)
+    pe.wait_ge(S.e0, nl)
+    pe.matmul(T.b0[:, :], T.exr[:, 0:B], T.exr[:, B:B + 512], False, True).then_inc(S.pe0, 1)
+    pe.wait_ge(S.e1, nl)
+    pe.matmul(T.b1[:, :], T.exr[:, 0:B], T.exr[:, B + 512:B + 1024], False, True).then_inc(S.pe1, 1)
+    seen = ["e1"]
+    for i, (xa, j, sem, cnt) in enumerate(terms):
+        for (s, n) in ((sem, cnt), ("lt%d" % corder.index(j // 4), 16)):
+            if s not in seen:
+                seen.append(s)
+                pe.wait_ge(S[s], n)
+        mm = pe.matmul(T.b2[:, 0:B], xa, T.dts[:, j * B:(j + 1) * B], i == 0, i == len(terms) - 1)
+    mm.then_inc(S.pe2, 1)
+
+    ve.wait_ge(S.pe0, 1)
+    ve.tensor_copy(T.ps[:, 0:512], T.b0[:, :]).then_inc(S.ev0, 1)
+    ve.wait_ge(S.pe1, 1)
+    ve.tensor_copy(T.ps[:, 512:896], T.b1[:, 0:384]).then_inc(S.ev1, 1)
+    acc = T.b1[:, 384:512]
+    for k in range(1, Q):
+        if k == 5:
+            ve.wait_ge(S.pe2, 1)
+            ve.tensor_copy(T.dwo[:, :], T.b2[:, 0:B]).then_inc(S.dwv, 1)
+        ve.wait_ge(S["p%d" % ((q - k) % Q)], len(pbits[k - 1]))
+        if k > 1:
+            ve.wait_ge(S.vs, k - 1)
+        ve.tensor_tensor(T.dxo[:, :] if k == Q - 1 else acc, acc, T.dl[:, (k - 1) * B:k * B],
+                         AluOpType.add).then_inc(S.vs, 1)
+
+    sent = 0
+    g.wait_ge(S.lx, 16)
+    ids = []
+    for k in range(1, Q):
+        rid, pid, _ = topo.addr(peers[k])
+        ids.append(DstId(rid=rid, pnc=pid))
+    g.remote_dma_fused([RemoteDMATransfer(dst_ids=ids, dma_engine_mask=off, remote_sem=S["x%d" % q],
+                                          srcs=[T.exs[:, XO:XO + B]],
+                                          dsts=[T.xl[:, (k - 1) * B:k * B] for k in range(1, Q)])], local_sem=S.sent)
+    sent += ne
+    g.wait_ge(S.lw, 16)
+    g.wait_ge(S.lp0, n_p0)
+    h = B + 512
+    g.remote_dma(T.exr[:, 0:h], T.exs[:, 0:h], S.e0, S.sent, ppid, prid, onl)
+    g.wait_ge(S.lp1, n_p1)
+    g.remote_dma(T.exr[:, h:HALF], T.exs[:, h:HALF], S.e1, S.sent, ppid, prid, onl)
+    g.sem_inc(S.gate, 1)
+    sent += 2 * nl
+    for (lo, hi, sem) in ((1, 5, "fa"), (5, Q, "fb")):
+        for k in range(lo, hi):
+            g.wait_ge(S["x%d" % ((q - k) % Q)], ne)
+        g.remote_dma(T.xf[:, (lo - 1) * B:(hi - 1) * B], T.xl[:, (lo - 1) * B:(hi - 1) * B], S[sem], S.sent,
+                     ppid, prid, onl)
+        sent += nl
+    for (lo, hi, sem) in ((0, 4, "ev0"), (4, Q - 1, "ev1")):
+        g.wait_ge(S[sem], 1)
+        trs = []
+        for t in range(lo, hi):
+            rid, pid, _ = topo.addr(peers[t + 1])
+            trs.append(RemoteDMATransfer(dst_ids=[DstId(rid=rid, pnc=pid)], dma_engine_mask=_mk(pbits[t]),
+                                         remote_sem=S["p%d" % q], srcs=[T.ps[:, t * B:(t + 1) * B]],
+                                         dsts=[T.dl[:, t * B:(t + 1) * B]]))
+            sent += len(pbits[t])
+        g.remote_dma_fused(trs, local_sem=S.sent)
+    g.wait_ge(S.sent, sent)
+    g.wait_ge(S.sdx, 16)
+    g.wait_ge(S.sdw, 16)

@@ -2,17 +2,19 @@ from concourse.bass import DstId, RemoteDMATransfer
 from concourse.mybir import AluOpType
 
 B = 128
-NB = 8
-XO = B + NB * B
-HALF = XO + B
+STAGE = ((0, 2), (2, 5), (5, 8))
+NH = 3
 
 SCRATCH = {
-    "exs": ("sbuf", [128, HALF], "float32"),
-    "exr": ("sbuf", [128, HALF], "float32"),
-    "dyo": ("sbuf", [128, NB * B], "float32"),
+    "xs": ("sbuf", [128, B], "float32"),
+    "xp": ("sbuf", [128, B], "float32"),
+    "exs": ("sbuf", [128, 9 * B], "float32"),
+    "exr": ("sbuf", [128, 9 * B], "float32"),
+    "dyo": ("sbuf", [128, 8 * B], "float32"),
     "dts": ("sbuf", [128, 16 * B], "float32"),
     "xl": ("sbuf", [128, 7 * B], "float32"),
-    "xf": ("sbuf", [128, 7 * B], "float32"),
+    "xf0": ("sbuf", [128, 7 * B], "float32"),
+    "xf1": ("sbuf", [128, 7 * B], "float32"),
     "ps": ("sbuf", [128, 7 * B], "float32"),
     "dl": ("sbuf", [128, 7 * B], "float32"),
     "dxo": ("sbuf", [128, B], "float32"),
@@ -20,9 +22,11 @@ SCRATCH = {
     "b0": ("psum", [128, 512], "float32"),
     "b1": ("psum", [128, 512], "float32"),
     "b2": ("psum", [128, 512], "float32"),
+    "bw": ("psum", [128, 512], "float32"),
 }
-SEMAPHORES = (["lx", "lw", "lp0", "lp1", "lo0", "lo1", "lt0", "lt1", "lt2", "lt3", "gate", "e0", "e1", "fa", "fb",
-               "pe0", "pe1", "pe2", "ev0", "ev1", "vs", "dwv", "sdx", "sdw", "sent"]
+SEMAPHORES = (["lx", "lw", "lp0", "lp1", "lo0", "lo1", "lt0", "lt1", "lt2", "lt3", "gate", "e0", "e1", "e2",
+               "pe0", "pe1", "pe2", "pew", "ev0", "ev1", "ev2", "vs", "dwv", "sdx", "sdw", "sent"]
+              + ["f%d%d" % (d, k) for d in range(2) for k in range(1, 8)]
               + ["x%d" % i for i in range(8)] + ["p%d" % i for i in range(8)])
 
 
@@ -37,42 +41,96 @@ def _mk(bs):
     return m
 
 
-def _runs(ranks, lo, hi):
-    out, t = [], lo
-    while t < hi:
+def _runs(ranks):
+    out, t = [], 0
+    while t < len(ranks):
         n = 1
-        while t + n < hi and ranks[t + n] == ranks[t] + n:
+        while t + n < len(ranks) and ranks[t + n] == ranks[t] + n:
             n += 1
         out.append((t, ranks[t], n))
         t += n
+    if len(out) == 1:
+        t, r, n = out[0]
+        out = [(t, r, n // 2), (t + n // 2, r + n // 2, n - n // 2)]
     return out
 
 
 def rank_program(g, core, T, topo):
     rank = T.rank_of(core)
-    if rank is None:
-        return
     S = T.sem
-    sy, sc, pe, ve = g.sync, g.scalar, g.tensor, g.vector
     cores = list(T.cores)
     chips = []
     for c in cores:
         if topo.chip(c) not in chips:
             chips.append(topo.chip(c))
+    if topo.chip(core) not in chips:
+        return
     Q = len(chips)
     q = chips.index(topo.chip(core))
+    every = range(topo.CORES_PER_CHIP * topo.CHIPS)
 
     def at(qi, die):
         return [c for c in cores if topo.chip(c) == chips[qi % Q] and topo.die(c) == die][0]
 
-    partner = [c for c in cores if topo.chip(c) == topo.chip(core) and c != core][0]
-    peers = [at(q + k, topo.die(core)) for k in range(Q)]
-    ppeers = [at(q + k, topo.die(partner)) for k in range(Q)]
+    def idles(qi, die):
+        return [c for c in every if topo.chip(c) == chips[qi % Q] and topo.die(c) == die
+                and T.rank_of(c) is None][0:NH]
+
+    def idle(qi, die, k):
+        li = idles(qi, die)
+        return li[(k - 1) % len(li)]
+
+    def other(c):
+        return [o for o in cores if topo.chip(o) == topo.chip(c) and o != c][0]
+
+    def xdst(c):
+        qc = chips.index(topo.chip(c))
+        return [idle(qc + k, topo.die(c), k) for k in range(1, Q)] + [other(c)]
+
+    def xmask(c):
+        m = topo.mask(c, other(c))
+        for d in xdst(c):
+            assert topo.may_write(c, d)
+            m &= topo.mask(c, d)
+        return m
+
+    def did(c):
+        rid, pid, _ = topo.addr(c)
+        return DstId(rid=rid, pnc=pid)
+
+    def fmask(h):
+        m = -1
+        for c in cores:
+            if topo.chip(c) == topo.chip(h):
+                m = topo.mask(h, c) if m < 0 else m & topo.mask(h, c)
+        return m
+
+    if rank is None:
+        d = topo.die(core)
+        mine = [k for k in range(1, Q) if idle(q, d, k) == core]
+        if not mine:
+            return
+        two = [c for c in cores if topo.chip(c) == topo.chip(core)]
+        m = fmask(core)
+        for k in mine:
+            g.wait_ge(S["x%d" % ((q - k) % Q)], len(_bits(xmask(at(q - k, d)))))
+            g.remote_dma_fused([RemoteDMATransfer(dst_ids=[did(c) for c in two], dma_engine_mask=m,
+                                                  remote_sem=S["f%d%d" % (d, k)],
+                                                  srcs=[T.xl[:, (k - 1) * B:k * B]],
+                                                  dsts=[T["xf%d" % d][:, (k - 1) * B:k * B] for c in two])],
+                               local_sem=S.sent)
+        g.wait_ge(S.sent, len(mine) * len(_bits(m)))
+        return
+
+    sy, sc, pe, ve = g.sync, g.scalar, g.tensor, g.vector
+    partner = other(core)
+    dme, dpa = topo.die(core), topo.die(partner)
+    peers = [at(q + k, dme) for k in range(Q)]
     order = list(range(1, Q)) + [0]
     own_r = [T.rank_of(peers[k]) for k in order]
-    par_r = [T.rank_of(ppeers[k]) for k in order]
+    par_r = [T.rank_of(at(q + k, dpa)) for k in order]
 
-    off = topo.mask(core, partner)
+    off = xmask(core)
     for k in range(1, Q):
         assert topo.may_write(core, peers[k])
         off &= topo.mask(core, peers[k])
@@ -82,21 +140,24 @@ def rank_program(g, core, T, topo):
     ob = _bits(off)
     ne, nl = len(ob), len(_bits(onl))
     e4 = ne // 4
-    pbits = [ob[i * e4:(i + 1) * e4] for i in range(4)] + [ob[0:2 * e4], ob[2 * e4:3 * e4], ob[3 * e4:4 * e4]]
+    two_way = [ob[0:2 * e4], ob[2 * e4:4 * e4]]
+    pbits = two_way + [ob[0:2 * e4], ob[2 * e4:3 * e4], ob[3 * e4:4 * e4]] + two_way
     prid, ppid, _ = topo.addr(partner)
+    banks = [T.b0, T.b1, T.b2]
 
-    def load(qu, dst, base, ranks, lo, hi, sem):
-        rs = _runs(ranks, lo, hi)
-        for (t, r, n) in rs:
-            qu.dma_start(dst[:, base + t * B:base + (t + n) * B], T.dy[:, r * B:(r + n) * B]).then_inc(S[sem], 16)
-        return 16 * len(rs)
+    def load(qus, dst, base, ranks, sems):
+        cnt = [0, 0]
+        for i, (t, r, n) in enumerate(_runs(ranks)):
+            qus[i % 2].dma_start(dst[:, base + t * B:base + (t + n) * B],
+                                 T.dy[:, r * B:(r + n) * B]).then_inc(S[sems[i % 2]], 16)
+            cnt[i % 2] += 16
+        return cnt
 
-    terms = [(T.exs[:, XO:XO + B], rank, "lx", 16)]
+    terms = [(T.xs[:, :], rank, "lx", 16), (T.xp[:, :], T.rank_of(partner), "x%d" % q, len(_bits(xmask(partner))))]
     for k in range(1, Q):
-        terms.append((T.xl[:, (k - 1) * B:k * B], T.rank_of(peers[Q - k]), "x%d" % ((q - k) % Q), ne))
-    terms.append((T.exr[:, XO:XO + B], T.rank_of(partner), "e1", nl))
-    for k in range(1, Q):
-        terms.append((T.xf[:, (k - 1) * B:k * B], T.rank_of(ppeers[Q - k]), "fa" if k <= 4 else "fb", nl))
+        for d in (dme, dpa):
+            terms.append((T["xf%d" % d][:, (k - 1) * B:k * B], T.rank_of(at(q - k, d)), "f%d%d" % (d, k),
+                          len(_bits(fmask(idle(q, d, k))))))
     corder = []
     for t in terms:
         if t[1] // 4 not in corder:
@@ -106,14 +167,12 @@ def rank_program(g, core, T, topo):
         c = corder[i]
         qu.dma_start(T.dts[:, c * 512:(c + 1) * 512], T.dyt[:, c * 512:(c + 1) * 512]).then_inc(S["lt%d" % i], 16)
 
-    sy.dma_start(T.exs[:, XO:XO + B], T.x[:, :]).then_inc(S.lx, 16)
+    sy.dma_start(T.xs[:, :], T.x[:, :]).then_inc(S.lx, 16)
     sc.dma_start(T.exs[:, 0:B], T.wt[:, :]).then_inc(S.lw, 16)
-    n_p0 = load(sy, T.exs, B, par_r, 0, 4, "lp0")
-    n_p1 = load(sc, T.exs, B, par_r, 4, 8, "lp1")
-    n_o0 = load(sy, T.dyo, 0, own_r, 0, 4, "lo0")
-    n_o1 = load(sc, T.dyo, 0, own_r, 4, 8, "lo1")
-    load_t(sy, 0)
-    load_t(sc, 1)
+    n_p = load((sy, sc), T.exs, B, par_r, ("lp0", "lp1"))
+    n_o = load((sc, sy), T.dyo, 0, own_r, ("lo0", "lo1"))
+    load_t(sc, 0)
+    load_t(sy, 1)
     sy.wait_ge(S.gate, 1)
     load_t(sy, 2)
     sc.wait_ge(S.gate, 1)
@@ -124,32 +183,33 @@ def rank_program(g, core, T, topo):
     sc.dma_start(T.dw[:, :], T.dwo[:, :]).then_inc(S.sdw, 16)
 
     pe.wait_ge(S.lw, 16)
-    pe.wait_ge(S.lo0, n_o0)
-    pe.matmul(T.b0[:, :], T.exs[:, 0:B], T.dyo[:, 0:512], True, False)
-    pe.wait_ge(S.lo1, n_o1)
-    pe.matmul(T.b1[:, :], T.exs[:, 0:B], T.dyo[:, 512:1024], True, False)
-    pe.wait_ge(S.e0, nl)
-    pe.matmul(T.b0[:, :], T.exr[:, 0:B], T.exr[:, B:B + 512], False, True).then_inc(S.pe0, 1)
-    pe.wait_ge(S.e1, nl)
-    pe.matmul(T.b1[:, :], T.exr[:, 0:B], T.exr[:, B + 512:B + 1024], False, True).then_inc(S.pe1, 1)
-    seen = ["e1"]
+    pe.wait_ge(S.lo0, n_o[0])
+    pe.wait_ge(S.lo1, n_o[1])
+    for i, (lo, hi) in enumerate(STAGE):
+        pe.matmul(banks[i][:, 0:(hi - lo) * B], T.exs[:, 0:B], T.dyo[:, lo * B:hi * B], True, False)
+    for i, (lo, hi) in enumerate(STAGE):
+        pe.wait_ge(S["e%d" % i], nl)
+        pe.matmul(banks[i][:, 0:(hi - lo) * B], T.exr[:, 0:B], T.exr[:, (lo + 1) * B:(hi + 1) * B], False,
+                  True).then_inc(S["pe%d" % i], 1)
+    seen = []
     for i, (xa, j, sem, cnt) in enumerate(terms):
         for (s, n) in ((sem, cnt), ("lt%d" % corder.index(j // 4), 16)):
             if s not in seen:
                 seen.append(s)
                 pe.wait_ge(S[s], n)
-        mm = pe.matmul(T.b2[:, 0:B], xa, T.dts[:, j * B:(j + 1) * B], i == 0, i == len(terms) - 1)
-    mm.then_inc(S.pe2, 1)
+        mm = pe.matmul(T.bw[:, 0:B], xa, T.dts[:, j * B:(j + 1) * B], i == 0, i == len(terms) - 1)
+    mm.then_inc(S.pew, 1)
 
-    ve.wait_ge(S.pe0, 1)
-    ve.tensor_copy(T.ps[:, 0:512], T.b0[:, :]).then_inc(S.ev0, 1)
-    ve.wait_ge(S.pe1, 1)
-    ve.tensor_copy(T.ps[:, 512:896], T.b1[:, 0:384]).then_inc(S.ev1, 1)
-    acc = T.b1[:, 384:512]
+    for i, (lo, hi) in enumerate(STAGE):
+        hi = min(hi, Q - 1)
+        ve.wait_ge(S["pe%d" % i], 1)
+        ve.tensor_copy(T.ps[:, lo * B:hi * B], banks[i][:, 0:(hi - lo) * B]).then_inc(S["ev%d" % i], 1)
+    lo = STAGE[-1][0]
+    acc = banks[-1][:, (Q - 1 - lo) * B:(Q - lo) * B]
     for k in range(1, Q):
-        if k == 5:
-            ve.wait_ge(S.pe2, 1)
-            ve.tensor_copy(T.dwo[:, :], T.b2[:, 0:B]).then_inc(S.dwv, 1)
+        if k == lo + 1:
+            ve.wait_ge(S.pew, 1)
+            ve.tensor_copy(T.dwo[:, :], T.bw[:, 0:B]).then_inc(S.dwv, 1)
         ve.wait_ge(S["p%d" % ((q - k) % Q)], len(pbits[k - 1]))
         if k > 1:
             ve.wait_ge(S.vs, k - 1)
@@ -158,34 +218,24 @@ def rank_program(g, core, T, topo):
 
     sent = 0
     g.wait_ge(S.lx, 16)
-    ids = []
-    for k in range(1, Q):
-        rid, pid, _ = topo.addr(peers[k])
-        ids.append(DstId(rid=rid, pnc=pid))
-    g.remote_dma_fused([RemoteDMATransfer(dst_ids=ids, dma_engine_mask=off, remote_sem=S["x%d" % q],
-                                          srcs=[T.exs[:, XO:XO + B]],
-                                          dsts=[T.xl[:, (k - 1) * B:k * B] for k in range(1, Q)])], local_sem=S.sent)
-    sent += ne
+    g.remote_dma_fused([RemoteDMATransfer(dst_ids=[did(c) for c in xdst(core)], dma_engine_mask=xmask(core),
+                                          remote_sem=S["x%d" % q], srcs=[T.xs[:, :]],
+                                          dsts=[T.xl[:, (k - 1) * B:k * B] for k in range(1, Q)] + [T.xp[:, :]])],
+                       local_sem=S.sent)
+    sent += len(_bits(xmask(core)))
     g.wait_ge(S.lw, 16)
-    g.wait_ge(S.lp0, n_p0)
-    h = B + 512
-    g.remote_dma(T.exr[:, 0:h], T.exs[:, 0:h], S.e0, S.sent, ppid, prid, onl)
-    g.wait_ge(S.lp1, n_p1)
-    g.remote_dma(T.exr[:, h:HALF], T.exs[:, h:HALF], S.e1, S.sent, ppid, prid, onl)
-    g.sem_inc(S.gate, 1)
-    sent += 2 * nl
-    for (lo, hi, sem) in ((1, 5, "fa"), (5, Q, "fb")):
-        for k in range(lo, hi):
-            g.wait_ge(S["x%d" % ((q - k) % Q)], ne)
-        g.remote_dma(T.xf[:, (lo - 1) * B:(hi - 1) * B], T.xl[:, (lo - 1) * B:(hi - 1) * B], S[sem], S.sent,
-                     ppid, prid, onl)
+    g.wait_ge(S.lp0, n_p[0])
+    g.wait_ge(S.lp1, n_p[1])
+    for i, (lo, hi) in enumerate(STAGE):
+        a = 0 if i == 0 else (lo + 1) * B
+        g.remote_dma(T.exr[:, a:(hi + 1) * B], T.exs[:, a:(hi + 1) * B], S["e%d" % i], S.sent, ppid, prid, onl)
         sent += nl
-    for (lo, hi, sem) in ((0, 4, "ev0"), (4, Q - 1, "ev1")):
-        g.wait_ge(S[sem], 1)
+    g.sem_inc(S.gate, 1)
+    for i, (lo, hi) in enumerate(STAGE):
+        g.wait_ge(S["ev%d" % i], 1)
         trs = []
-        for t in range(lo, hi):
-            rid, pid, _ = topo.addr(peers[t + 1])
-            trs.append(RemoteDMATransfer(dst_ids=[DstId(rid=rid, pnc=pid)], dma_engine_mask=_mk(pbits[t]),
+        for t in range(lo, min(hi, Q - 1)):
+            trs.append(RemoteDMATransfer(dst_ids=[did(peers[t + 1])], dma_engine_mask=_mk(pbits[t]),
                                          remote_sem=S["p%d" % q], srcs=[T.ps[:, t * B:(t + 1) * B]],
                                          dsts=[T.dl[:, t * B:(t + 1) * B]]))
             sent += len(pbits[t])

from concourse.bass import DstId, RemoteDMATransfer
from concourse.mybir import AluOpType

B = 128
STAGE = ((0, 2), (2, 5), (5, 8))
NH = 3

SCRATCH = {
    "xs": ("sbuf", [128, B], "float32"),
    "xp": ("sbuf", [128, B], "float32"),
    "exs": ("sbuf", [128, 9 * B], "float32"),
    "exr": ("sbuf", [128, 9 * B], "float32"),
    "dyo": ("sbuf", [128, 8 * B], "float32"),
    "dts": ("sbuf", [128, 16 * B], "float32"),
    "xl": ("sbuf", [128, 7 * B], "float32"),
    "xf0": ("sbuf", [128, 7 * B], "float32"),
    "xf1": ("sbuf", [128, 7 * B], "float32"),
    "ps": ("sbuf", [128, 7 * B], "float32"),
    "dl": ("sbuf", [128, 7 * B], "float32"),
    "dxo": ("sbuf", [128, B], "float32"),
    "dwo": ("sbuf", [128, B], "float32"),
    "b0": ("psum", [128, 512], "float32"),
    "b1": ("psum", [128, 512], "float32"),
    "b2": ("psum", [128, 512], "float32"),
    "bw": ("psum", [128, 512], "float32"),
}
SEMAPHORES = (["lx", "lw", "lp0", "lp1", "lo0", "lo1", "lt0", "lt1", "lt2", "lt3", "gate", "e0", "e1", "e2",
               "pe0", "pe1", "pe2", "pew", "ev0", "ev1", "ev2", "vs", "dwv", "sdx", "sdw", "sent"]
              + ["f%d%d" % (d, k) for d in range(2) for k in range(1, 8)]
              + ["x%d" % i for i in range(8)] + ["p%d" % i for i in range(8)])


def _bits(m):
    return [b for b in range(m.bit_length()) if (m >> b) & 1]


def _mk(bs):
    m = 0
    for b in bs:
        m |= 1 << b
    return m


def _runs(ranks):
    out, t = [], 0
    while t < len(ranks):
        n = 1
        while t + n < len(ranks) and ranks[t + n] == ranks[t] + n:
            n += 1
        out.append((t, ranks[t], n))
        t += n
    if len(out) == 1:
        t, r, n = out[0]
        out = [(t, r, n // 2), (t + n // 2, r + n // 2, n - n // 2)]
    return out


def rank_program(g, core, T, topo):
    rank = T.rank_of(core)
    S = T.sem
    cores = list(T.cores)
    chips = []
    for c in cores:
        if topo.chip(c) not in chips:
            chips.append(topo.chip(c))
    if topo.chip(core) not in chips:
        return
    Q = len(chips)
    q = chips.index(topo.chip(core))
    every = range(topo.CORES_PER_CHIP * topo.CHIPS)

    def at(qi, die):
        return [c for c in cores if topo.chip(c) == chips[qi % Q] and topo.die(c) == die][0]

    def idles(qi, die):
        return [c for c in every if topo.chip(c) == chips[qi % Q] and topo.die(c) == die
                and T.rank_of(c) is None][0:NH]

    def idle(qi, die, k):
        li = idles(qi, die)
        return li[(k - 1) % len(li)]

    def other(c):
        return [o for o in cores if topo.chip(o) == topo.chip(c) and o != c][0]

    def xdst(c):
        qc = chips.index(topo.chip(c))
        return [idle(qc + k, topo.die(c), k) for k in range(1, Q)] + [other(c)]

    def xmask(c):
        m = topo.mask(c, other(c))
        for d in xdst(c):
            assert topo.may_write(c, d)
            m &= topo.mask(c, d)
        return m

    def did(c):
        rid, pid, _ = topo.addr(c)
        return DstId(rid=rid, pnc=pid)

    def fmask(h):
        m = -1
        for c in cores:
            if topo.chip(c) == topo.chip(h):
                m = topo.mask(h, c) if m < 0 else m & topo.mask(h, c)
        return m

    if rank is None:
        d = topo.die(core)
        mine = [k for k in range(1, Q) if idle(q, d, k) == core]
        if not mine:
            return
        two = [c for c in cores if topo.chip(c) == topo.chip(core)]
        m = fmask(core)
        for k in mine:
            g.wait_ge(S["x%d" % ((q - k) % Q)], len(_bits(xmask(at(q - k, d)))))
            g.remote_dma_fused([RemoteDMATransfer(dst_ids=[did(c) for c in two], dma_engine_mask=m,
                                                  remote_sem=S["f%d%d" % (d, k)],
                                                  srcs=[T.xl[:, (k - 1) * B:k * B]],
                                                  dsts=[T["xf%d" % d][:, (k - 1) * B:k * B] for c in two])],
                               local_sem=S.sent)
        g.wait_ge(S.sent, len(mine) * len(_bits(m)))
        return

    sy, sc, pe, ve = g.sync, g.scalar, g.tensor, g.vector
    partner = other(core)
    dme, dpa = topo.die(core), topo.die(partner)
    peers = [at(q + k, dme) for k in range(Q)]
    order = list(range(1, Q)) + [0]
    own_r = [T.rank_of(peers[k]) for k in order]
    par_r = [T.rank_of(at(q + k, dpa)) for k in order]

    off = xmask(core)
    for k in range(1, Q):
        assert topo.may_write(core, peers[k])
        off &= topo.mask(core, peers[k])
    onl = topo.mask(core, partner) & ~off
    if len(_bits(onl)) not in (1, 2, 4, 8, 16):
        onl = topo.mask(core, partner)
    ob = _bits(off)
    ne, nl = len(ob), len(_bits(onl))
    e4 = ne // 4
    two_way = [ob[0:2 * e4], ob[2 * e4:4 * e4]]
    pbits = two_way + [ob[0:2 * e4], ob[2 * e4:3 * e4], ob[3 * e4:4 * e4]] + two_way
    prid, ppid, _ = topo.addr(partner)
    banks = [T.b0, T.b1, T.b2]

    def load(qus, dst, base, ranks, sems):
        cnt = [0, 0]
        for i, (t, r, n) in enumerate(_runs(ranks)):
            qus[i % 2].dma_start(dst[:, base + t * B:base + (t + n) * B],
                                 T.dy[:, r * B:(r + n) * B]).then_inc(S[sems[i % 2]], 16)
            cnt[i % 2] += 16
        return cnt

    terms = [(T.xs[:, :], rank, "lx", 16), (T.xp[:, :], T.rank_of(partner), "x%d" % q, len(_bits(xmask(partner))))]
    for k in range(1, Q):
        for d in (dme, dpa):
            terms.append((T["xf%d" % d][:, (k - 1) * B:k * B], T.rank_of(at(q - k, d)), "f%d%d" % (d, k),
                          len(_bits(fmask(idle(q, d, k))))))
    corder = []
    for t in terms:
        if t[1] // 4 not in corder:
            corder.append(t[1] // 4)

    def load_t(qu, i):
        c = corder[i]
        qu.dma_start(T.dts[:, c * 512:(c + 1) * 512], T.dyt[:, c * 512:(c + 1) * 512]).then_inc(S["lt%d" % i], 16)

    sy.dma_start(T.xs[:, :], T.x[:, :]).then_inc(S.lx, 16)
    sc.dma_start(T.exs[:, 0:B], T.wt[:, :]).then_inc(S.lw, 16)
    n_p = load((sy, sc), T.exs, B, par_r, ("lp0", "lp1"))
    n_o = load((sc, sy), T.dyo, 0, own_r, ("lo0", "lo1"))
    load_t(sc, 0)
    load_t(sy, 1)
    sy.wait_ge(S.gate, 1)
    load_t(sy, 2)
    sc.wait_ge(S.gate, 1)
    load_t(sc, 3)
    sy.wait_ge(S.vs, Q - 1)
    sy.dma_start(T.dx[:, :], T.dxo[:, :]).then_inc(S.sdx, 16)
    sc.wait_ge(S.dwv, 1)
    sc.dma_start(T.dw[:, :], T.dwo[:, :]).then_inc(S.sdw, 16)

    pe.wait_ge(S.lw, 16)
    pe.wait_ge(S.lo0, n_o[0])
    pe.wait_ge(S.lo1, n_o[1])
    for i, (lo, hi) in enumerate(STAGE):
        pe.matmul(banks[i][:, 0:(hi - lo) * B], T.exs[:, 0:B], T.dyo[:, lo * B:hi * B], True, False)
    for i, (lo, hi) in enumerate(STAGE):
        pe.wait_ge(S["e%d" % i], nl)
        pe.matmul(banks[i][:, 0:(hi - lo) * B], T.exr[:, 0:B], T.exr[:, (lo + 1) * B:(hi + 1) * B], False,
                  True).then_inc(S["pe%d" % i], 1)
    seen = []
    for i, (xa, j, sem, cnt) in enumerate(terms):
        for (s, n) in ((sem, cnt), ("lt%d" % corder.index(j // 4), 16)):
            if s not in seen:
                seen.append(s)
                pe.wait_ge(S[s], n)
        mm = pe.matmul(T.bw[:, 0:B], xa, T.dts[:, j * B:(j + 1) * B], i == 0, i == len(terms) - 1)
    mm.then_inc(S.pew, 1)

    for i, (lo, hi) in enumerate(STAGE):
        hi = min(hi, Q - 1)
        ve.wait_ge(S["pe%d" % i], 1)
        ve.tensor_copy(T.ps[:, lo * B:hi * B], banks[i][:, 0:(hi - lo) * B]).then_inc(S["ev%d" % i], 1)
    lo = STAGE[-1][0]
    acc = banks[-1][:, (Q - 1 - lo) * B:(Q - lo) * B]
    for k in range(1, Q):
        if k == lo + 1:
            ve.wait_ge(S.pew, 1)
            ve.tensor_copy(T.dwo[:, :], T.bw[:, 0:B]).then_inc(S.dwv, 1)
        ve.wait_ge(S["p%d" % ((q - k) % Q)], len(pbits[k - 1]))
        if k > 1:
            ve.wait_ge(S.vs, k - 1)
        ve.tensor_tensor(T.dxo[:, :] if k == Q - 1 else acc, acc, T.dl[:, (k - 1) * B:k * B],
                         AluOpType.add).then_inc(S.vs, 1)

    sent = 0
    g.wait_ge(S.lx, 16)
    g.remote_dma_fused([RemoteDMATransfer(dst_ids=[did(c) for c in xdst(core)], dma_engine_mask=xmask(core),
                                          remote_sem=S["x%d" % q], srcs=[T.xs[:, :]],
                                          dsts=[T.xl[:, (k - 1) * B:k * B] for k in range(1, Q)] + [T.xp[:, :]])],
                       local_sem=S.sent)
    sent += len(_bits(xmask(core)))
    g.wait_ge(S.lw, 16)
    g.wait_ge(S.lp0, n_p[0])
    g.wait_ge(S.lp1, n_p[1])
    for i, (lo, hi) in enumerate(STAGE):
        a = 0 if i == 0 else (lo + 1) * B
        g.remote_dma(T.exr[:, a:(hi + 1) * B], T.exs[:, a:(hi + 1) * B], S["e%d" % i], S.sent, ppid, prid, onl)
        sent += nl
    g.sem_inc(S.gate, 1)
    for i, (lo, hi) in enumerate(STAGE):
        g.wait_ge(S["ev%d" % i], 1)
        trs = []
        for t in range(lo, min(hi, Q - 1)):
            trs.append(RemoteDMATransfer(dst_ids=[did(peers[t + 1])], dma_engine_mask=_mk(pbits[t]),
                                         remote_sem=S["p%d" % q], srcs=[T.ps[:, t * B:(t + 1) * B]],
                                         dsts=[T.dl[:, t * B:(t + 1) * B]]))
            sent += len(pbits[t])
        g.remote_dma_fused(trs, local_sem=S.sent)
    g.wait_ge(S.sent, sent)
    g.wait_ge(S.sdx, 16)
    g.wait_ge(S.sdw, 16)
